import numpy as np
import ml_dtypes


def mxq(x, axis, fmt="e4m3"):
    dtype, down = {"e4m3": (ml_dtypes.float8_e4m3fn, 7), "e5m2": (ml_dtypes.float8_e5m2, 14)}[fmt]
    v = np.moveaxis(np.asarray(x, np.float32).astype(ml_dtypes.bfloat16).astype(np.float64), axis, -1)
    blocks = v.reshape(v.shape[:-1] + (-1, 32))
    amax = np.abs(blocks).max(-1, keepdims=True)
    byte = np.maximum(np.where(amax > 0, np.frexp(amax)[1] - 1 + 127, 0) - down, 1)
    scale = np.exp2(byte - 127.0)
    codes = (blocks / scale).astype(np.float32).astype(dtype).astype(np.float64)
    return np.moveaxis((codes * scale).reshape(v.shape), -1, axis)


WIDE = False


def mx_kscale(k):
    if not WIDE:
        return np.ones(k)
    levels = np.array([10, -10, 5, -5, 0])
    if k % 512:
        return np.exp2(np.random.permutation(np.resize(levels, k // 32))).repeat(32)
    a = np.empty((k // 512, 16))
    for p in range(k // 512):
        a[p, :8] = np.random.permutation(np.resize(levels, 8))
        for g in range(8):
            far = levels[np.abs(levels - a[p, g]) >= 10]
            a[p, g + 8] = far[np.random.randint(len(far))]
    return np.exp2(a.ravel()).repeat(32)


def f64(x):
    return np.asarray(x).astype(np.float64)


def striped(idx):
    return np.tile(idx.reshape(-1, 16).T, (8, 1)).astype(np.uint16)


def unstriped(offs):
    return offs[:16].T.reshape(-1).astype(np.int64)


E2M1 = np.array([0.0, 0.5, 1.0, 1.5, 2.0, 3.0, 4.0, 6.0, -0.0, -0.5, -1.0, -1.5, -2.0, -3.0, -4.0, -6.0])


def pack_weight(w, fmt):
    k, n = w.shape
    w = f64(np.asarray(w, np.float32).astype(ml_dtypes.bfloat16)).reshape(k // 32, 32, n)
    amax = np.abs(w).max(1)
    if fmt == "e4m3":
        byte = np.frexp(amax)[1] - 1 + 127 - 7
    else:
        mant, ex = np.frexp(amax / 6.0)
        byte = np.where(mant > 0.5, ex, ex - 1) + 127
    byte = np.clip(np.where(amax > 0, byte, 1), 1, 254)
    scaled = (w * np.exp2(127.0 - byte)[:, None, :]).reshape(k, n).astype(np.float32)
    by_word = np.ascontiguousarray(scaled.reshape(k // 512, 128, 4, n).transpose(0, 1, 3, 2))
    if fmt == "e4m3":
        words = by_word.astype(ml_dtypes.float8_e4m3fn).view(np.uint8)
    else:
        c = by_word.astype(ml_dtypes.float4_e2m1fn).view(np.uint8) & 0xF
        words = (c[..., 0::2] | (c[..., 1::2] << 4)).reshape(k // 512, 128, 2 * n)
    return np.ascontiguousarray(words), np.ascontiguousarray(byte.astype(np.uint8).reshape(k // 512, 16, n))


def unpack_weight(words, scales, fmt):
    g, _, n = scales.shape
    words = np.ascontiguousarray(words).reshape(g, 128, n, -1)
    if fmt == "e4m3":
        vals = words.view(ml_dtypes.float8_e4m3fn).astype(np.float64)
    else:
        nib = np.empty((g, 128, n, 4), np.uint8)
        nib[..., 0::2] = words & 0xF
        nib[..., 1::2] = words >> 4
        vals = E2M1[nib]
    vals = vals * np.repeat(np.exp2(scales.astype(np.float64) - 127.0), 8, axis=1)[..., None]
    return vals.transpose(0, 1, 3, 2).reshape(g * 512, n)


def gelu(v):
    return 0.5 * v * (1.0 + np.tanh(np.sqrt(2.0 / np.pi) * (v + 0.044715 * v**3)))


K, H, N, T, S, P, P2 = 1024, 1024, 512, 4096, 2048, 1024, 512

def setup_inputs():
    n = np.random.standard_normal
    s = mx_kscale(K)[:, None]
    u = mx_kscale(H)[:, None]
    tab_words, tab_scales = pack_weight(n((K, T)) * s, "e4m3")
    w1_words, w1_scales = pack_weight(1.5 * n((K, H)) / np.sqrt(K) / s, "e2m1")
    return {
        "tab_words": tab_words, "tab_scales": tab_scales,
        "offs": striped(np.random.permutation(T)[:S]),
        "pos1": striped(np.random.permutation(S)[:P]),
        "pos2": striped(np.random.permutation(S)[:P]),
        "pos3": striped(np.random.permutation(P)[:P2]),
        "pos4": striped(np.random.permutation(S)[:P2]),
        "w1_words": w1_words, "w1_scales": w1_scales,
        "gain": (np.exp(0.3 * n(H)) * u[:, 0]).astype(np.float32),
        "prior": (1.2 * np.exp(0.3 * n(H)) / u[:, 0]).astype(np.float32),
        "w2": (n((H, N)) / np.sqrt(H) / u).astype(np.float32),
        "rel": np.exp(0.5 * n((N, P2))).astype(np.float32),
    }

def reference(tab_words, tab_scales, offs, pos1, pos2, pos3, pos4, w1_words, w1_scales, gain, prior, w2, rel):
    v = unpack_weight(tab_words, tab_scales, "e4m3")[:, unstriped(offs)]
    w1 = unpack_weight(w1_words, w1_scales, "e2m1")
    h = f64(gain)[:, None] * np.tanh(w1.T @ v)
    a1 = np.maximum(h[:, unstriped(pos1)], h[:, unstriped(pos2)])
    x = a1[:, unstriped(pos3)]
    tune = f64(prior)[:, None] * h[:, unstriped(pos4)]
    a2 = x * tune + x
    y = mxq(f64(w2), 0, "e4m3").T @ mxq(a2, 0, "e4m3")
    return f64(rel) * y

@@ -1,0 +1,235 @@
+from contextlib import ExitStack
+
+import concourse.mybir as mybir
+from concourse.masks import make_identity
+
+K, H, N, T, S, PAIRS, KEPT = 1024, 1024, 512, 4096, 2048, 1024, 512
+FLOPS = 2 * K * H * S + 2 * H * N * KEPT
+
+F32 = mybir.dt.float32
+BF16 = mybir.dt.bfloat16
+I32 = mybir.dt.int32
+U32 = mybir.dt.uint32
+U16 = mybir.dt.uint16
+U8 = mybir.dt.uint8
+FP8X4 = mybir.dt.float8_e4m3fn_x4
+FP4X4 = mybir.dt.float4_e2m1fn_x4
+ACT = mybir.ActivationFunctionType
+ALU = mybir.AluOpType
+
+P = 128
+BANK = 512
+SLICES = H // P
+FIRST_CHUNKS = [(0, 512), (512, 1024), (1024, 1536), (1536, 1792), (1792, 2048)]
+BANK_CHUNKS = [(0, 512), (512, 1024), (1024, 1536), (1536, 2048)]
+TAIL_CHUNKS = [(0, 256), (256, 384), (384, 512)]
+
+
+def interleave(nc, grouped, rows):
+    nc.scalar.copy(
+        out=grouped.rearrange("p (c i t) -> p c t i", i=4, t=4),
+        in_=rows.rearrange("p t (c i) -> p c t i", i=4),
+    )
+
+
+def tile_list_disputed_melody_scores_kernel(
+    tc, tab_words, tab_scales, offs, pos1, pos2, pos3, pos4, w1_words, w1_scales, gain, prior, w2, rel, out
+):
+    nc = tc.nc
+    with ExitStack() as ctx:
+        keep = ctx.enter_context(tc.tile_pool(name="keep", bufs=1))
+        ring = ctx.enter_context(tc.tile_pool(name="ring", bufs=2))
+        psum = ctx.enter_context(tc.psum_pool(name="psum", bufs=1))
+
+        idx = keep.tile([P, S // 16], U16, name="idx")
+        p1 = keep.tile([P, PAIRS // 16], U16, name="p1")
+        p2 = keep.tile([P, PAIRS // 16], U16, name="p2")
+        p3 = keep.tile([P, KEPT // 16], U16, name="p3")
+        p4 = keep.tile([P, KEPT // 16], U16, name="p4")
+        tab_rows = keep.tile([P, T], U8, name="tab_rows", align_bytes=64)
+        tab = [keep.tile([P, T], I32, name="tab%d" % a, align_bytes=64) for a in range(2)]
+        w1_raw = keep.tile([P, 2, 2 * H], U8, name="w1_raw", tag="w_raw", align_bytes=64)
+        w1s_raw = keep.tile([P, 2, H], U8, name="w1s_raw", tag="side_raw", align_bytes=64)
+        v_plane = [keep.tile([P, S], U8, name="v_plane%d" % a, align_bytes=64) for a in range(2)]
+        rows = keep.tile([P, 2 * P], F32, name="rows")
+        ident = keep.tile([P, P], F32, name="ident")
+        out_bank = [psum.tile([P, BANK], F32, name="out_bank%d" % i) for i in range(4)]
+
+        nc.vector.memset(w1s_raw[:].rearrange("p a c -> p (a c)").bitcast(I32), 0)
+        nc.vector.memset(tab_rows[32:64, :].bitcast(I32), 0)
+        nc.vector.memset(tab_rows[64:128, :].bitcast(I32), 0)
+        for a in range(2):
+            nc.vector.memset(v_plane[a][:].bitcast(I32), 0)
+        nc.gpsimd.memset(rows[:], 0.0)
+        make_identity(nc, ident[:])
+
+        nc.sync.dma_start(idx[:], offs)
+        nc.sync.dma_start(tab_rows[0:32, :].bitcast(I32), tab_scales.rearrange("a q t -> (a q) t").bitcast(I32))
+        nc.sync.dma_start(p1[:], pos1)
+        nc.sync.dma_start(p2[:], pos2)
+        nc.sync.dma_start(p4[:], pos4)
+        nc.sync.dma_start(p3[:], pos3)
+        nc.sync.dma_start(tab[0][:], tab_words[0].rearrange("p t i -> p (t i)").bitcast(I32))
+        nc.sync.dma_start(w1_raw[:].bitcast(I32), w1_words.rearrange("a p c -> p a c").bitcast(I32))
+        nc.sync.dma_start(tab[1][:], tab_words[1].rearrange("p t i -> p (t i)").bitcast(I32))
+        for quad in range(4):
+            nc.scalar.dma_start(
+                w1s_raw[32 * quad : 32 * quad + 4, :, :].bitcast(I32),
+                w1_scales[:, 4 * quad : 4 * quad + 4, :].rearrange("a r c -> r a c").bitcast(I32),
+            )
+        for first, vec in ((0, gain), (4, prior)):
+            nc.scalar.dma_start(
+                rows[first : first + 4, :].rearrange("t (m u) -> t m u", u=8),
+                vec.rearrange("(m t u) -> t m u", t=4, u=8),
+            )
+
+        picked_rows = keep.tile([P, S], U8, name="picked_rows", align_bytes=64)
+        nc.vector.tensor_copy(picked_rows[:], tab_rows[:].indirect(idx[:]))
+        for a in range(2):
+            for quad in range(4):
+                src = 16 * a + 4 * quad
+                nc.sync.dma_start(
+                    v_plane[a][32 * quad : 32 * quad + 4, :].bitcast(I32),
+                    picked_rows[src : src + 4, :].bitcast(I32),
+                )
+
+        per_row = keep.tile([P, 2, 8], F32, name="per_row")
+        for b in range(2):
+            nc.tensor.transpose(out_bank[3][:, P * b : P * (b + 1)], rows[:, P * b : P * (b + 1)], ident[:])
+        nc.scalar.copy(out=per_row[:], in_=out_bank[3][:, 0 : 2 * P].rearrange("p (b x) -> p b x", b=2)[:, :, 0:8])
+
+        v_words = [keep.tile([P, S], U32, name="v_words%d" % a, align_bytes=64) for a in range(2)]
+        nc.vector.tensor_copy(v_words[0][:], tab[0][:].bitcast(U32).indirect(idx[:]))
+
+        w1_codes = [keep.tile([P, 2, 4, 2 * P], U8, name="w1_codes%d" % b, align_bytes=64) for b in range(2)]
+        w1_plane = [keep.tile([P, 2, 4, P], U8, name="w1_plane%d" % b, align_bytes=64) for b in range(2)]
+        for b in range(2):
+            nc.vector.tensor_copy(
+                out=w1_codes[b][:].bitcast(I32).rearrange("p a t (q w) -> p a t q w", w=4),
+                in_=w1_raw[:, :, H * b : H * (b + 1)].bitcast(I32).rearrange("p a (q t w) -> p a t q w", t=4, w=4),
+            )
+            nc.vector.tensor_copy(
+                out=w1_plane[b][:].bitcast(I32).rearrange("p a t (q w) -> p a t q w", w=2),
+                in_=w1s_raw[:, :, 512 * b : 512 * (b + 1)].bitcast(I32).rearrange("p a (q t w) -> p a t q w", t=4, w=2),
+            )
+
+        for lo, hi in FIRST_CHUNKS:
+            nc.vector.tensor_copy(v_words[1][:, lo:hi], tab[1][:].bitcast(U32).indirect(idx[:, lo // 16 : hi // 16]))
+
+        w2_raw = keep.tile([P, 2, 4, N], F32, name="w2_raw", tag="w_raw", align_bytes=64)
+        w2_rows = w2.rearrange("(b q t u) n -> b t q u n", b=2, t=4, u=8)
+        for b in range(2):
+            for t in range(4):
+                nc.sync.dma_start(w2_raw[:, b, t, :], w2_rows[b, t])
+        rel_sb = keep.tile([P, 4, KEPT], F32, name="rel_sb", tag="side_raw", align_bytes=64)
+        nc.sync.dma_start(rel_sb[:], rel.rearrange("(i p) j -> p i j", p=P))
+
+        def features(s):
+            b, t = divmod(s, 4)
+            th = ring.tile([P, S], F32, name="th", bufs=2)
+            h = ring.tile([P, S], F32, name="h", bufs=3)
+            g = per_row[:, b, t : t + 1]
+            for lo, hi in FIRST_CHUNKS if s == 0 else BANK_CHUNKS:
+                z = psum.tile([P, BANK], F32, name="z", bufs=4)
+                for a in range(2):
+                    nc.tensor.matmul_mx(
+                        out=z[:, 0 : hi - lo],
+                        lhsT=w1_codes[b][:, a, t, :].bitcast(FP4X4),
+                        lhsT_scale=w1_plane[b][:, a, t, :],
+                        rhs=v_words[a][:, lo:hi].bitcast(FP8X4),
+                        rhs_scale=v_plane[a][:, lo:hi],
+                        start=(a == 0),
+                        stop=(a == 1),
+                    )
+                nc.scalar.activation(out=th[:, lo:hi], in_=z[:, 0 : hi - lo], func=ACT.Tanh)
+                if s == 0:
+                    nc.vector.tensor_scalar(h[:, lo:hi], th[:, lo:hi], g, None, ALU.mult)
+            if s > 0:
+                nc.scalar.activation(out=h[:], in_=th[:], func=ACT.Copy, scale=g)
+            return h
+
+        both = [keep.tile([P, 2 * PAIRS], F32, name="both%d" % i) for i in range(2)]
+        a1 = [keep.tile([P, PAIRS], F32, name="a1_%d" % t) for t in range(4)]
+        lift = [keep.tile([P, KEPT], F32, name="lift%d" % t) for t in range(4)]
+
+        def pairs(s, h):
+            b, t = divmod(s, 4)
+            two = both[s % 2]
+            nc.vector.tensor_copy(two[:, 0:PAIRS], h[:].indirect(p1[:]))
+            nc.vector.tensor_copy(two[:, PAIRS : 2 * PAIRS], h[:].indirect(p2[:]))
+            h4 = ring.tile([P, KEPT], F32, name="h4")
+            nc.vector.tensor_copy(h4[:], h[:].indirect(p4[:]))
+            nc.vector.tensor_tensor(a1[t][:], two[:, 0:PAIRS], two[:, PAIRS : 2 * PAIRS], ALU.max)
+            nc.scalar.activation(out=lift[t][:], in_=h4[:], func=ACT.Copy, scale=per_row[:, b, 4 + t : 5 + t], bias=1.0)
+
+        def quantise(rows4, width, name):
+            grouped = keep.tile([P, 4 * width], BF16, name=name + "_bf", align_bytes=64)
+            codes = keep.tile([P, width], U32, name=name + "_codes", align_bytes=64)
+            plane = keep.tile([P, width], U8, name=name + "_plane", align_bytes=64)
+            interleave(nc, grouped[:], rows4)
+            nc.vector.quantize_mx(out=codes[:].bitcast(FP8X4), scales=plane[:], in_=grouped[:])
+            return codes, plane, grouped
+
+        def place(c, i):
+            lo, hi = TAIL_CHUNKS[c]
+            width = hi - lo
+            per_bank = BANK // width
+            first_bank = 4 * lo // BANK
+            return first_bank + i // per_bank, (i % per_bank) * width, i % per_bank == 0, i % per_bank == per_bank - 1
+
+        def scores(b, c, w2_q, a2_q, col):
+            lo, hi = TAIL_CHUNKS[c]
+            for i in range(4):
+                bank, at, first, last = place(c, i)
+                nc.tensor.matmul_mx(
+                    out=out_bank[bank][:, at : at + hi - lo],
+                    lhsT=w2_q[0][:, P * i : P * (i + 1)].bitcast(FP8X4),
+                    lhsT_scale=w2_q[1][:, P * i : P * (i + 1)],
+                    rhs=a2_q[0][:, col : col + hi - lo].bitcast(FP8X4),
+                    rhs_scale=a2_q[1][:, col : col + hi - lo],
+                    start=(b == 0 and first),
+                    stop=(b == 1 and last),
+                )
+
+        a2_first = keep.tile([P, 4, KEPT], F32, name="a2_first")
+        w2_q = []
+        h_next = features(0)
+        for s in range(SLICES):
+            h = h_next
+            if s + 1 < SLICES:
+                h_next = features(s + 1)
+            pairs(s, h)
+            if s < 4:
+                nc.vector.tensor_tensor(a2_first[:, s, :], a1[s][:].indirect(p3[:]), lift[s][:], ALU.mult)
+            if s in (1, 2):
+                w2_q.append(quantise(w2_raw[:, s - 1, :, :], N, "w2_%d" % (s - 1)))
+            if s == 3:
+                a2_q = quantise(a2_first[:], KEPT, "a2_first")
+                for c, (lo, hi) in enumerate(TAIL_CHUNKS):
+                    scores(0, c, w2_q[0], a2_q, lo)
+
+        out_rows = out.rearrange("(i p) j -> p i j", p=P)
+        a2_last = both[(SLICES - 1) % 2]
+        rounded = []
+        for c, (lo, hi) in enumerate(TAIL_CHUNKS):
+            width = hi - lo
+            room = a2_last[:, 4 * lo : 4 * hi] if c < 2 else rounded[0][:].bitcast(F32)
+            part = room.rearrange("p (t j) -> p t j", t=4)
+            for t in range(4):
+                nc.vector.tensor_tensor(
+                    part[:, t, :], a1[t][:].indirect(p3[:, lo // 16 : hi // 16]), lift[t][:, lo:hi], ALU.mult
+                )
+            a2_q = quantise(part, width, "a2_last%d" % c)
+            rounded.append(a2_q[2])
+            scores(1, c, w2_q[1], a2_q, 0)
+            per_bank = BANK // width
+            for i0 in range(0, 4, per_bank):
+                bank = place(c, i0)[0]
+                result = keep.tile([P, per_bank, width], F32, name="result%d" % bank)
+                nc.vector.tensor_tensor(
+                    result[:],
+                    out_bank[bank][:].rearrange("p (i j) -> p i j", i=per_bank),
+                    rel_sb[:, i0 : i0 + per_bank, lo:hi],
+                    ALU.mult,
+                )
+                nc.sync.dma_start(out_rows[:, i0 : i0 + per_bank, lo:hi], result[:])

@@ -55,13 +55,13 @@ def tile_list_disputed_melody_scores_kernel(
         ident = keep.tile([P, P], F32, name="ident")
         out_bank = [psum.tile([P, BANK], F32, name="out_bank%d" % i) for i in range(4)]
 
-        nc.vector.memset(w1s_raw[:].rearrange("p a c -> p (a c)").bitcast(I32), 0)
         nc.vector.memset(tab_rows[32:64, :].bitcast(I32), 0)
         nc.vector.memset(tab_rows[64:128, :].bitcast(I32), 0)
-        for a in range(2):
-            nc.vector.memset(v_plane[a][:].bitcast(I32), 0)
+        nc.gpsimd.memset(w1s_raw[:].rearrange("p a c -> p (a c)").bitcast(I32), 0)
         nc.gpsimd.memset(rows[:], 0.0)
         make_identity(nc, ident[:])
+        for a in range(2):
+            nc.gpsimd.memset(v_plane[a][:].bitcast(I32), 0)
 
         nc.sync.dma_start(idx[:], offs)
         nc.sync.dma_start(tab_rows[0:32, :].bitcast(I32), tab_scales.rearrange("a q t -> (a q) t").bitcast(I32))
@@ -104,11 +104,11 @@ def tile_list_disputed_melody_scores_kernel(
         w1_codes = [keep.tile([P, 2, 4, 2 * P], U8, name="w1_codes%d" % b, align_bytes=64) for b in range(2)]
         w1_plane = [keep.tile([P, 2, 4, P], U8, name="w1_plane%d" % b, align_bytes=64) for b in range(2)]
         for b in range(2):
-            nc.vector.tensor_copy(
+            nc.gpsimd.tensor_copy(
                 out=w1_codes[b][:].bitcast(I32).rearrange("p a t (q w) -> p a t q w", w=4),
                 in_=w1_raw[:, :, H * b : H * (b + 1)].bitcast(I32).rearrange("p a (q t w) -> p a t q w", t=4, w=4),
             )
-            nc.vector.tensor_copy(
+            nc.gpsimd.tensor_copy(
                 out=w1_plane[b][:].bitcast(I32).rearrange("p a t (q w) -> p a t q w", w=2),
                 in_=w1s_raw[:, :, 512 * b : 512 * (b + 1)].bitcast(I32).rearrange("p a (q t w) -> p a t q w", t=4, w=2),
             )
@@ -124,9 +124,12 @@ def tile_list_disputed_melody_scores_kernel(
         rel_sb = keep.tile([P, 4, KEPT], F32, name="rel_sb", tag="side_raw", align_bytes=64)
         nc.sync.dma_start(rel_sb[:], rel.rearrange("(i p) j -> p i j", p=P))
 
+        bent = [keep.tile([P, S], F32, name="bent%d" % i, align_bytes=64) for i in range(2)]
+        bent_first = keep.tile([P, S], F32, name="bent_first", align_bytes=64)
+
         def features(s):
             b, t = divmod(s, 4)
-            th = ring.tile([P, S], F32, name="th", bufs=2)
+            th = bent_first if s == 0 else bent[s % 2]
             h = ring.tile([P, S], F32, name="h", bufs=3)
             g = per_row[:, b, t : t + 1]
             for lo, hi in FIRST_CHUNKS if s == 0 else BANK_CHUNKS:
@@ -154,21 +157,31 @@ def tile_list_disputed_melody_scores_kernel(
 
         def pairs(s, h):
             b, t = divmod(s, 4)
-            two = both[s % 2]
-            nc.vector.tensor_copy(two[:, 0:PAIRS], h[:].indirect(p1[:]))
-            nc.vector.tensor_copy(two[:, PAIRS : 2 * PAIRS], h[:].indirect(p2[:]))
+            left = both[s % 2][:, 0:PAIRS]
+            right = both[s % 2][:, PAIRS : 2 * PAIRS]
             h4 = ring.tile([P, KEPT], F32, name="h4")
-            nc.vector.tensor_copy(h4[:], h[:].indirect(p4[:]))
-            nc.vector.tensor_tensor(a1[t][:], two[:, 0:PAIRS], two[:, PAIRS : 2 * PAIRS], ALU.max)
+            if s + 1 < SLICES:
+                nc.vector.tensor_copy(left, h[:].indirect(p1[:]))
+                nc.vector.tensor_copy(h4[:], h[:].indirect(p4[:]))
+                nc.vector.tensor_tensor(right, h[:].indirect(p2[:]), left, ALU.subtract)
+                nc.scalar.activation(out=right, in_=right, func=ACT.Relu)
+                nc.gpsimd.tensor_tensor(a1[t][:], left, right, ALU.add)
+            else:
+                nc.vector.tensor_copy(h4[:], h[:].indirect(p4[:]))
+                nc.vector.tensor_copy(left, h[:].indirect(p1[:]))
+                nc.vector.tensor_copy(right, h[:].indirect(p2[:]))
+                nc.vector.tensor_tensor(a1[t][:], left, right, ALU.max)
             nc.scalar.activation(out=lift[t][:], in_=h4[:], func=ACT.Copy, scale=per_row[:, b, 4 + t : 5 + t], bias=1.0)
 
-        def quantise(rows4, width, name):
-            grouped = keep.tile([P, 4 * width], BF16, name=name + "_bf", align_bytes=64)
+        def quantise(grouped, name):
+            width = grouped.shape[1] // 4
             codes = keep.tile([P, width], U32, name=name + "_codes", align_bytes=64)
             plane = keep.tile([P, width], U8, name=name + "_plane", align_bytes=64)
-            interleave(nc, grouped[:], rows4)
-            nc.vector.quantize_mx(out=codes[:].bitcast(FP8X4), scales=plane[:], in_=grouped[:])
-            return codes, plane, grouped
+            nc.vector.quantize_mx(out=codes[:].bitcast(FP8X4), scales=plane[:], in_=grouped)
+            return codes, plane
+
+        def kept(t, lo, hi, into):
+            nc.vector.tensor_tensor(into, a1[t][:].indirect(p3[:, lo // 16 : hi // 16]), lift[t][:, lo:hi], ALU.mult)
 
         def place(c, i):
             lo, hi = TAIL_CHUNKS[c]
@@ -192,35 +205,49 @@ def tile_list_disputed_melody_scores_kernel(
                 )
 
         a2_first = keep.tile([P, 4, KEPT], F32, name="a2_first")
-        w2_q = []
+        a2_wide = keep.tile([P, 4, 256], F32, name="a2_wide")
         h_next = features(0)
+        w2_low = bent_first[:, S // 2 : S].bitcast(BF16)
+        nc.gpsimd.tensor_scalar(
+            w2_low.rearrange("p (c t) -> p c t", t=4), w2_raw[:, 0, :, :].rearrange("p t c -> p c t"), 1.0, 0.0, ALU.mult, ALU.add
+        )
         for s in range(SLICES):
             h = h_next
             if s + 1 < SLICES:
                 h_next = features(s + 1)
             pairs(s, h)
             if s < 4:
-                nc.vector.tensor_tensor(a2_first[:, s, :], a1[s][:].indirect(p3[:]), lift[s][:], ALU.mult)
-            if s in (1, 2):
-                w2_q.append(quantise(w2_raw[:, s - 1, :, :], N, "w2_%d" % (s - 1)))
-            if s == 3:
-                a2_q = quantise(a2_first[:], KEPT, "a2_first")
+                kept(s, 0, KEPT, a2_first[:, s, :])
+            else:
+                kept(s - 4, 0, 256, a2_wide[:, s - 4, :])
+            if s == 0:
+                w2_q = [quantise(w2_low, "w2_low")]
+            if s == SLICES - 1:
+                late = bent[(SLICES - 1) % 2]
+                a2_low = late[:, 0 : S // 2].bitcast(BF16)
+                interleave(nc, a2_low, a2_first[:])
+                a2_q = quantise(a2_low, "a2_low")
                 for c, (lo, hi) in enumerate(TAIL_CHUNKS):
                     scores(0, c, w2_q[0], a2_q, lo)
+                w2_high = late[:, S // 2 : S].bitcast(BF16)
+                interleave(nc, w2_high, w2_raw[:, 1, :, :])
+                w2_q.append(quantise(w2_high, "w2_high"))
 
         out_rows = out.rearrange("(i p) j -> p i j", p=P)
-        a2_last = both[(SLICES - 1) % 2]
         rounded = []
         for c, (lo, hi) in enumerate(TAIL_CHUNKS):
             width = hi - lo
-            room = a2_last[:, 4 * lo : 4 * hi] if c < 2 else rounded[0][:].bitcast(F32)
-            part = room.rearrange("p (t j) -> p t j", t=4)
-            for t in range(4):
-                nc.vector.tensor_tensor(
-                    part[:, t, :], a1[t][:].indirect(p3[:, lo // 16 : hi // 16]), lift[t][:, lo:hi], ALU.mult
-                )
-            a2_q = quantise(part, width, "a2_last%d" % c)
-            rounded.append(a2_q[2])
+            if c == 0:
+                part = a2_wide[:]
+            else:
+                room = both[(SLICES - 1) % 2][:, 0 : 4 * width] if c == 1 else rounded[0][:].bitcast(F32)
+                part = room.rearrange("p (t j) -> p t j", t=4)
+                for t in range(4):
+                    kept(t, lo, hi, part[:, t, :])
+            grouped = keep.tile([P, 4 * width], BF16, name="a2_high%d" % c, align_bytes=64)
+            rounded.append(grouped)
+            interleave(nc, grouped[:], part)
+            a2_q = quantise(grouped[:], "a2_high%d" % c)
             scores(1, c, w2_q[1], a2_q, 0)
             per_bank = BANK // width
             for i0 in range(0, 4, per_bank):

@@ -59,12 +59,9 @@ def tile_list_disputed_melody_scores_kernel(
         nc.vector.memset(tab_rows[64:128, :].bitcast(I32), 0)
         nc.gpsimd.memset(w1s_raw[:].rearrange("p a c -> p (a c)").bitcast(I32), 0)
         nc.gpsimd.memset(rows[:], 0.0)
-        make_identity(nc, ident[:])
-        for a in range(2):
-            nc.gpsimd.memset(v_plane[a][:].bitcast(I32), 0)
 
         nc.sync.dma_start(idx[:], offs)
-        nc.sync.dma_start(tab_rows[0:32, :].bitcast(I32), tab_scales.rearrange("a q t -> (a q) t").bitcast(I32))
+        nc.scalar.dma_start(tab_rows[0:32, :].bitcast(I32), tab_scales.rearrange("a q t -> (a q) t").bitcast(I32))
         nc.sync.dma_start(p1[:], pos1)
         nc.sync.dma_start(p2[:], pos2)
         nc.sync.dma_start(p4[:], pos4)
@@ -73,22 +70,25 @@ def tile_list_disputed_melody_scores_kernel(
         nc.sync.dma_start(w1_raw[:].bitcast(I32), w1_words.rearrange("a p c -> p a c").bitcast(I32))
         nc.sync.dma_start(tab[1][:], tab_words[1].rearrange("p t i -> p (t i)").bitcast(I32))
         for quad in range(4):
-            nc.scalar.dma_start(
+            nc.gpsimd.dma_start(
                 w1s_raw[32 * quad : 32 * quad + 4, :, :].bitcast(I32),
                 w1_scales[:, 4 * quad : 4 * quad + 4, :].rearrange("a r c -> r a c").bitcast(I32),
             )
         for first, vec in ((0, gain), (4, prior)):
-            nc.scalar.dma_start(
+            nc.gpsimd.dma_start(
                 rows[first : first + 4, :].rearrange("t (m u) -> t m u", u=8),
                 vec.rearrange("(m t u) -> t m u", t=4, u=8),
             )
+
+        make_identity(nc, ident[:])
 
         picked_rows = keep.tile([P, S], U8, name="picked_rows", align_bytes=64)
         nc.vector.tensor_copy(picked_rows[:], tab_rows[:].indirect(idx[:]))
         for a in range(2):
             for quad in range(4):
                 src = 16 * a + 4 * quad
-                nc.sync.dma_start(
+                queue = nc.gpsimd if src == 28 else nc.sync
+                queue.dma_start(
                     v_plane[a][32 * quad : 32 * quad + 4, :].bitcast(I32),
                     picked_rows[src : src + 4, :].bitcast(I32),
                 )
@@ -151,27 +151,32 @@ def tile_list_disputed_melody_scores_kernel(
                 nc.scalar.activation(out=h[:], in_=th[:], func=ACT.Copy, scale=g)
             return h
 
-        both = [keep.tile([P, 2 * PAIRS], F32, name="both%d" % i) for i in range(2)]
+        lefts = [keep.tile([P, PAIRS], F32, name="left%d" % i) for i in range(2)]
+        rights = [keep.tile([P, PAIRS], F32, name="right%d" % t) for t in range(4)]
+        lift_last = keep.tile([P, KEPT], F32, name="lift_last")
         a1 = [keep.tile([P, PAIRS], F32, name="a1_%d" % t) for t in range(4)]
-        lift = [keep.tile([P, KEPT], F32, name="lift%d" % t) for t in range(4)]
+
+        def lift(s):
+            return lift_last[:] if s == SLICES - 1 else rights[s % 4][:, 0:KEPT]
 
         def pairs(s, h):
             b, t = divmod(s, 4)
-            left = both[s % 2][:, 0:PAIRS]
-            right = both[s % 2][:, PAIRS : 2 * PAIRS]
+            left = lefts[s % 2][:]
+            right = rights[t][:]
             h4 = ring.tile([P, KEPT], F32, name="h4")
             if s + 1 < SLICES:
                 nc.vector.tensor_copy(left, h[:].indirect(p1[:]))
                 nc.vector.tensor_copy(h4[:], h[:].indirect(p4[:]))
                 nc.vector.tensor_tensor(right, h[:].indirect(p2[:]), left, ALU.subtract)
-                nc.scalar.activation(out=right, in_=right, func=ACT.Relu)
-                nc.gpsimd.tensor_tensor(a1[t][:], left, right, ALU.add)
+                excess = bent[(s + 1) % 2][:, PAIRS : 2 * PAIRS]
+                nc.scalar.activation(out=excess, in_=right, func=ACT.Relu)
+                nc.gpsimd.tensor_tensor(a1[t][:], left, excess, ALU.add)
             else:
                 nc.vector.tensor_copy(h4[:], h[:].indirect(p4[:]))
                 nc.vector.tensor_copy(left, h[:].indirect(p1[:]))
                 nc.vector.tensor_copy(right, h[:].indirect(p2[:]))
                 nc.vector.tensor_tensor(a1[t][:], left, right, ALU.max)
-            nc.scalar.activation(out=lift[t][:], in_=h4[:], func=ACT.Copy, scale=per_row[:, b, 4 + t : 5 + t], bias=1.0)
+            nc.scalar.activation(out=lift(s), in_=h4[:], func=ACT.Copy, scale=per_row[:, b, 4 + t : 5 + t], bias=1.0)
 
         def quantise(grouped, name):
             width = grouped.shape[1] // 4
@@ -180,8 +185,8 @@ def tile_list_disputed_melody_scores_kernel(
             nc.vector.quantize_mx(out=codes[:].bitcast(FP8X4), scales=plane[:], in_=grouped)
             return codes, plane
 
-        def kept(t, lo, hi, into):
-            nc.vector.tensor_tensor(into, a1[t][:].indirect(p3[:, lo // 16 : hi // 16]), lift[t][:, lo:hi], ALU.mult)
+        def kept(s, lo, hi, into):
+            nc.vector.tensor_tensor(into, a1[s % 4][:].indirect(p3[:, lo // 16 : hi // 16]), lift(s)[:, lo:hi], ALU.mult)
 
         def place(c, i):
             lo, hi = TAIL_CHUNKS[c]
@@ -219,7 +224,7 @@ def tile_list_disputed_melody_scores_kernel(
             if s < 4:
                 kept(s, 0, KEPT, a2_first[:, s, :])
             else:
-                kept(s - 4, 0, 256, a2_wide[:, s - 4, :])
+                kept(s, 0, 256, a2_wide[:, s - 4, :])
             if s == 0:
                 w2_q = [quantise(w2_low, "w2_low")]
             if s == SLICES - 1:
@@ -240,10 +245,10 @@ def tile_list_disputed_melody_scores_kernel(
             if c == 0:
                 part = a2_wide[:]
             else:
-                room = both[(SLICES - 1) % 2][:, 0 : 4 * width] if c == 1 else rounded[0][:].bitcast(F32)
+                room = late[:, 0 : 4 * width] if c == 1 else rounded[0][:].bitcast(F32)
                 part = room.rearrange("p (t j) -> p t j", t=4)
                 for t in range(4):
-                    kept(t, lo, hi, part[:, t, :])
+                    kept(4 + t, lo, hi, part[:, t, :])
             grouped = keep.tile([P, 4 * width], BF16, name="a2_high%d" % c, align_bytes=64)
             rounded.append(grouped)
             interleave(nc, grouped[:], part)

@@ -48,10 +48,10 @@ def tile_list_disputed_melody_scores_kernel(
         p4 = keep.tile([P, KEPT // 16], U16, name="p4")
         tab_rows = keep.tile([P, T], U8, name="tab_rows", align_bytes=64)
         tab = [keep.tile([P, T], I32, name="tab%d" % a, align_bytes=64) for a in range(2)]
-        w1_raw = keep.tile([P, 2, 2 * H], U8, name="w1_raw", tag="w_raw", align_bytes=64)
+        w1_raw = keep.tile([P, 2, 2 * H], U8, name="w1_raw", align_bytes=64)
         w1s_raw = keep.tile([P, 2, H], U8, name="w1s_raw", tag="side_raw", align_bytes=64)
         v_plane = [keep.tile([P, S], U8, name="v_plane%d" % a, align_bytes=64) for a in range(2)]
-        rows = keep.tile([P, 2 * P], F32, name="rows")
+        rows = keep.tile([P, 2 * P], F32, name="rows", tag="w_raw", align_bytes=64)
         ident = keep.tile([P, P], F32, name="ident")
         out_bank = [psum.tile([P, BANK], F32, name="out_bank%d" % i) for i in range(4)]
 
@@ -103,15 +103,12 @@ def tile_list_disputed_melody_scores_kernel(
 
         w1_codes = [keep.tile([P, 2, 4, 2 * P], U8, name="w1_codes%d" % b, align_bytes=64) for b in range(2)]
         w1_plane = [keep.tile([P, 2, 4, P], U8, name="w1_plane%d" % b, align_bytes=64) for b in range(2)]
-        for b in range(2):
-            nc.gpsimd.tensor_copy(
-                out=w1_codes[b][:].bitcast(I32).rearrange("p a t (q w) -> p a t q w", w=4),
-                in_=w1_raw[:, :, H * b : H * (b + 1)].bitcast(I32).rearrange("p a (q t w) -> p a t q w", t=4, w=4),
-            )
-            nc.gpsimd.tensor_copy(
-                out=w1_plane[b][:].bitcast(I32).rearrange("p a t (q w) -> p a t q w", w=2),
-                in_=w1s_raw[:, :, 512 * b : 512 * (b + 1)].bitcast(I32).rearrange("p a (q t w) -> p a t q w", t=4, w=2),
-            )
+        for b, ts in ((0, slice(0, 1)), (0, slice(1, 4)), (1, slice(0, 4))):
+            for dealt, raw, run in ((w1_codes[b], w1_raw, 4), (w1_plane[b], w1s_raw, 2)):
+                words = raw[:].bitcast(I32).rearrange("p a (b q t w) -> p b a t q w", b=2, t=4, w=run)
+                nc.gpsimd.tensor_copy(
+                    out=dealt[:].bitcast(I32).rearrange("p a t (q w) -> p a t q w", w=run)[:, :, ts], in_=words[:, b, :, ts]
+                )
 
         for lo, hi in FIRST_CHUNKS:
             nc.vector.tensor_copy(v_words[1][:, lo:hi], tab[1][:].bitcast(U32).indirect(idx[:, lo // 16 : hi // 16]))
@@ -124,12 +121,13 @@ def tile_list_disputed_melody_scores_kernel(
         rel_sb = keep.tile([P, 4, KEPT], F32, name="rel_sb", tag="side_raw", align_bytes=64)
         nc.sync.dma_start(rel_sb[:], rel.rearrange("(i p) j -> p i j", p=P))
 
-        bent = [keep.tile([P, S], F32, name="bent%d" % i, align_bytes=64) for i in range(2)]
-        bent_first = keep.tile([P, S], F32, name="bent_first", align_bytes=64)
+        low = [keep.tile([P, S // 2], F32, name="low%d" % i, align_bytes=64) for i in range(3)]
+        high = [keep.tile([P, 3 * S // 4 if i == 1 else S // 2], F32, name="high%d" % i, align_bytes=64) for i in range(3)]
+        bent = [(low[i][:], high[i][:, 0 : S // 2]) for i in range(3)]
 
         def features(s):
             b, t = divmod(s, 4)
-            th = bent_first if s == 0 else bent[s % 2]
+            halves = bent[2] if s == 0 else bent[s % 2]
             h = ring.tile([P, S], F32, name="h", bufs=3)
             g = per_row[:, b, t : t + 1]
             for lo, hi in FIRST_CHUNKS if s == 0 else BANK_CHUNKS:
@@ -144,17 +142,26 @@ def tile_list_disputed_melody_scores_kernel(
                         start=(a == 0),
                         stop=(a == 1),
                     )
-                nc.scalar.activation(out=th[:, lo:hi], in_=z[:, 0 : hi - lo], func=ACT.Tanh)
+                half, at = divmod(lo, S // 2)
+                th = halves[half][:, at : at + hi - lo]
+                nc.scalar.activation(out=th, in_=z[:, 0 : hi - lo], func=ACT.Tanh)
                 if s == 0:
-                    nc.vector.tensor_scalar(h[:, lo:hi], th[:, lo:hi], g, None, ALU.mult)
+                    nc.vector.tensor_scalar(h[:, lo:hi], th, g, None, ALU.mult)
             if s > 0:
-                nc.scalar.activation(out=h[:], in_=th[:], func=ACT.Copy, scale=g)
+                for half in range(2):
+                    nc.scalar.activation(
+                        out=h[:, half * S // 2 : (half + 1) * S // 2], in_=halves[half], func=ACT.Copy, scale=g
+                    )
             return h
 
         lefts = [keep.tile([P, PAIRS], F32, name="left%d" % i) for i in range(2)]
         rights = [keep.tile([P, PAIRS], F32, name="right%d" % t) for t in range(4)]
         lift_last = keep.tile([P, KEPT], F32, name="lift_last")
-        a1 = [keep.tile([P, PAIRS], F32, name="a1_%d" % t) for t in range(4)]
+        a1_ring = [keep.tile([P, PAIRS], F32, name="a1_%d" % t) for t in range(4)]
+        late = bent[(SLICES - 1) % 2]
+
+        def a1(s):
+            return late[0] if s == SLICES - 1 else a1_ring[s % 4][:]
 
         def lift(s):
             return lift_last[:] if s == SLICES - 1 else rights[s % 4][:, 0:KEPT]
@@ -168,14 +175,13 @@ def tile_list_disputed_melody_scores_kernel(
                 nc.vector.tensor_copy(left, h[:].indirect(p1[:]))
                 nc.vector.tensor_copy(h4[:], h[:].indirect(p4[:]))
                 nc.vector.tensor_tensor(right, h[:].indirect(p2[:]), left, ALU.subtract)
-                excess = bent[(s + 1) % 2][:, PAIRS : 2 * PAIRS]
+                excess = bent[(s + 1) % 2][1 if s in (0, SLICES - 2) else 0]
                 nc.scalar.activation(out=excess, in_=right, func=ACT.Relu)
-                nc.gpsimd.tensor_tensor(a1[t][:], left, excess, ALU.add)
+                nc.gpsimd.tensor_tensor(a1(s), left, excess, ALU.add)
             else:
                 nc.vector.tensor_copy(h4[:], h[:].indirect(p4[:]))
                 nc.vector.tensor_copy(left, h[:].indirect(p1[:]))
                 nc.vector.tensor_copy(right, h[:].indirect(p2[:]))
-                nc.vector.tensor_tensor(a1[t][:], left, right, ALU.max)
             nc.scalar.activation(out=lift(s), in_=h4[:], func=ACT.Copy, scale=per_row[:, b, 4 + t : 5 + t], bias=1.0)
 
         def quantise(grouped, name):
@@ -186,7 +192,7 @@ def tile_list_disputed_melody_scores_kernel(
             return codes, plane
 
         def kept(s, lo, hi, into):
-            nc.vector.tensor_tensor(into, a1[s % 4][:].indirect(p3[:, lo // 16 : hi // 16]), lift(s)[:, lo:hi], ALU.mult)
+            nc.vector.tensor_tensor(into, a1(s).indirect(p3[:, lo // 16 : hi // 16]), lift(s)[:, lo:hi], ALU.mult)
 
         def place(c, i):
             lo, hi = TAIL_CHUNKS[c]
@@ -210,9 +216,9 @@ def tile_list_disputed_melody_scores_kernel(
                 )
 
         a2_first = keep.tile([P, 4, KEPT], F32, name="a2_first")
-        a2_wide = keep.tile([P, 4, 256], F32, name="a2_wide")
+        parts = [keep.tile([P, 4, hi - lo], F32, name="a2_part%d" % lo)[:] for lo, hi in TAIL_CHUNKS[:2]]
         h_next = features(0)
-        w2_low = bent_first[:, S // 2 : S].bitcast(BF16)
+        w2_low = bent[2][1].bitcast(BF16)
         nc.gpsimd.tensor_scalar(
             w2_low.rearrange("p (c t) -> p c t", t=4), w2_raw[:, 0, :, :].rearrange("p t c -> p c t"), 1.0, 0.0, ALU.mult, ALU.add
         )
@@ -221,38 +227,38 @@ def tile_list_disputed_melody_scores_kernel(
             if s + 1 < SLICES:
                 h_next = features(s + 1)
             pairs(s, h)
-            if s < 4:
-                kept(s, 0, KEPT, a2_first[:, s, :])
-            else:
-                kept(s, 0, 256, a2_wide[:, s - 4, :])
-            if s == 0:
-                w2_q = [quantise(w2_low, "w2_low")]
             if s == SLICES - 1:
-                late = bent[(SLICES - 1) % 2]
-                a2_low = late[:, 0 : S // 2].bitcast(BF16)
+                a2_low = late[0].bitcast(BF16)
                 interleave(nc, a2_low, a2_first[:])
                 a2_q = quantise(a2_low, "a2_low")
                 for c, (lo, hi) in enumerate(TAIL_CHUNKS):
                     scores(0, c, w2_q[0], a2_q, lo)
-                w2_high = late[:, S // 2 : S].bitcast(BF16)
-                interleave(nc, w2_high, w2_raw[:, 1, :, :])
-                w2_q.append(quantise(w2_high, "w2_high"))
+                nc.vector.tensor_tensor(a1(s), lefts[s % 2][:], rights[s % 4][:], ALU.max)
+            if s < 4:
+                kept(s, 0, KEPT, a2_first[:, s, :])
+            else:
+                for part, (lo, hi) in zip(parts, TAIL_CHUNKS):
+                    kept(s, lo, hi, part[:, s - 4, :])
+            if s == 0:
+                w2_q = [quantise(w2_low, "w2_low")]
+
+        w2_high = late[1].bitcast(BF16)
+        interleave(nc, w2_high, w2_raw[:, 1, :, :])
+        w2_q.append(quantise(w2_high, "w2_high"))
 
         out_rows = out.rearrange("(i p) j -> p i j", p=P)
-        rounded = []
         for c, (lo, hi) in enumerate(TAIL_CHUNKS):
             width = hi - lo
             if c == 0:
-                part = a2_wide[:]
+                grouped = high[1][:, S // 2 : S // 2 + 2 * width].bitcast(BF16)
             else:
-                room = late[:, 0 : 4 * width] if c == 1 else rounded[0][:].bitcast(F32)
-                part = room.rearrange("p (t j) -> p t j", t=4)
+                grouped = keep.tile([P, 4 * width], BF16, name="a2_high%d" % c, align_bytes=64)[:]
+            if c == 2:
+                parts.append(high[1][:, S // 2 - 2 * width : S // 2 + 2 * width].rearrange("p (t j) -> p t j", t=4))
                 for t in range(4):
-                    kept(4 + t, lo, hi, part[:, t, :])
-            grouped = keep.tile([P, 4 * width], BF16, name="a2_high%d" % c, align_bytes=64)
-            rounded.append(grouped)
-            interleave(nc, grouped[:], part)
-            a2_q = quantise(grouped[:], "a2_high%d" % c)
+                    kept(4 + t, lo, hi, parts[2][:, t, :])
+            interleave(nc, grouped, parts[c])
+            a2_q = quantise(grouped, "a2_high%d" % c)
             scores(1, c, w2_q[1], a2_q, 0)
             per_bank = BANK // width
             for i0 in range(0, 4, per_bank):

from contextlib import ExitStack

import concourse.mybir as mybir
from concourse.masks import make_identity

K, H, N, T, S, PAIRS, KEPT = 1024, 1024, 512, 4096, 2048, 1024, 512
FLOPS = 2 * K * H * S + 2 * H * N * KEPT

F32 = mybir.dt.float32
BF16 = mybir.dt.bfloat16
I32 = mybir.dt.int32
U32 = mybir.dt.uint32
U16 = mybir.dt.uint16
U8 = mybir.dt.uint8
FP8X4 = mybir.dt.float8_e4m3fn_x4
FP4X4 = mybir.dt.float4_e2m1fn_x4
ACT = mybir.ActivationFunctionType
ALU = mybir.AluOpType

P = 128
BANK = 512
SLICES = H // P
FIRST_CHUNKS = [(0, 512), (512, 1024), (1024, 1536), (1536, 1792), (1792, 2048)]
BANK_CHUNKS = [(0, 512), (512, 1024), (1024, 1536), (1536, 2048)]
TAIL_CHUNKS = [(0, 256), (256, 384), (384, 512)]


def interleave(nc, grouped, rows):
    nc.scalar.copy(
        out=grouped.rearrange("p (c i t) -> p c t i", i=4, t=4),
        in_=rows.rearrange("p t (c i) -> p c t i", i=4),
    )


def tile_list_disputed_melody_scores_kernel(
    tc, tab_words, tab_scales, offs, pos1, pos2, pos3, pos4, w1_words, w1_scales, gain, prior, w2, rel, out
):
    nc = tc.nc
    with ExitStack() as ctx:
        keep = ctx.enter_context(tc.tile_pool(name="keep", bufs=1))
        ring = ctx.enter_context(tc.tile_pool(name="ring", bufs=2))
        psum = ctx.enter_context(tc.psum_pool(name="psum", bufs=1))

        idx = keep.tile([P, S // 16], U16, name="idx")
        p1 = keep.tile([P, PAIRS // 16], U16, name="p1")
        p2 = keep.tile([P, PAIRS // 16], U16, name="p2")
        p3 = keep.tile([P, KEPT // 16], U16, name="p3")
        p4 = keep.tile([P, KEPT // 16], U16, name="p4")
        tab_rows = keep.tile([P, T], U8, name="tab_rows", align_bytes=64)
        tab = [keep.tile([P, T], I32, name="tab%d" % a, align_bytes=64) for a in range(2)]
        w1_raw = keep.tile([P, 2, 2 * H], U8, name="w1_raw", align_bytes=64)
        w1s_raw = keep.tile([P, 2, H], U8, name="w1s_raw", tag="side_raw", align_bytes=64)
        v_plane = [keep.tile([P, S], U8, name="v_plane%d" % a, align_bytes=64) for a in range(2)]
        rows = keep.tile([P, 2 * P], F32, name="rows", tag="w_raw", align_bytes=64)
        ident = keep.tile([P, P], F32, name="ident")
        out_bank = [psum.tile([P, BANK], F32, name="out_bank%d" % i) for i in range(4)]

        nc.vector.memset(tab_rows[32:64, :].bitcast(I32), 0)
        nc.vector.memset(tab_rows[64:128, :].bitcast(I32), 0)
        nc.gpsimd.memset(w1s_raw[:].rearrange("p a c -> p (a c)").bitcast(I32), 0)
        nc.gpsimd.memset(rows[:], 0.0)

        nc.sync.dma_start(idx[:], offs)
        nc.scalar.dma_start(tab_rows[0:32, :].bitcast(I32), tab_scales.rearrange("a q t -> (a q) t").bitcast(I32))
        nc.sync.dma_start(p1[:], pos1)
        nc.sync.dma_start(p2[:], pos2)
        nc.sync.dma_start(p4[:], pos4)
        nc.sync.dma_start(p3[:], pos3)
        nc.sync.dma_start(tab[0][:], tab_words[0].rearrange("p t i -> p (t i)").bitcast(I32))
        nc.sync.dma_start(w1_raw[:].bitcast(I32), w1_words.rearrange("a p c -> p a c").bitcast(I32))
        nc.sync.dma_start(tab[1][:], tab_words[1].rearrange("p t i -> p (t i)").bitcast(I32))
        for quad in range(4):
            nc.gpsimd.dma_start(
                w1s_raw[32 * quad : 32 * quad + 4, :, :].bitcast(I32),
                w1_scales[:, 4 * quad : 4 * quad + 4, :].rearrange("a r c -> r a c").bitcast(I32),
            )
        for first, vec in ((0, gain), (4, prior)):
            nc.gpsimd.dma_start(
                rows[first : first + 4, :].rearrange("t (m u) -> t m u", u=8),
                vec.rearrange("(m t u) -> t m u", t=4, u=8),
            )

        make_identity(nc, ident[:])

        picked_rows = keep.tile([P, S], U8, name="picked_rows", align_bytes=64)
        nc.vector.tensor_copy(picked_rows[:], tab_rows[:].indirect(idx[:]))
        for a in range(2):
            for quad in range(4):
                src = 16 * a + 4 * quad
                queue = nc.gpsimd if src == 28 else nc.sync
                queue.dma_start(
                    v_plane[a][32 * quad : 32 * quad + 4, :].bitcast(I32),
                    picked_rows[src : src + 4, :].bitcast(I32),
                )

        per_row = keep.tile([P, 2, 8], F32, name="per_row")
        for b in range(2):
            nc.tensor.transpose(out_bank[3][:, P * b : P * (b + 1)], rows[:, P * b : P * (b + 1)], ident[:])
        nc.scalar.copy(out=per_row[:], in_=out_bank[3][:, 0 : 2 * P].rearrange("p (b x) -> p b x", b=2)[:, :, 0:8])

        v_words = [keep.tile([P, S], U32, name="v_words%d" % a, align_bytes=64) for a in range(2)]
        nc.vector.tensor_copy(v_words[0][:], tab[0][:].bitcast(U32).indirect(idx[:]))

        w1_codes = [keep.tile([P, 2, 4, 2 * P], U8, name="w1_codes%d" % b, align_bytes=64) for b in range(2)]
        w1_plane = [keep.tile([P, 2, 4, P], U8, name="w1_plane%d" % b, align_bytes=64) for b in range(2)]
        for b, ts in ((0, slice(0, 1)), (0, slice(1, 4)), (1, slice(0, 4))):
            for dealt, raw, run in ((w1_codes[b], w1_raw, 4), (w1_plane[b], w1s_raw, 2)):
                words = raw[:].bitcast(I32).rearrange("p a (b q t w) -> p b a t q w", b=2, t=4, w=run)
                nc.gpsimd.tensor_copy(
                    out=dealt[:].bitcast(I32).rearrange("p a t (q w) -> p a t q w", w=run)[:, :, ts], in_=words[:, b, :, ts]
                )

        for lo, hi in FIRST_CHUNKS:
            nc.vector.tensor_copy(v_words[1][:, lo:hi], tab[1][:].bitcast(U32).indirect(idx[:, lo // 16 : hi // 16]))

        w2_raw = keep.tile([P, 2, 4, N], F32, name="w2_raw", tag="w_raw", align_bytes=64)
        w2_rows = w2.rearrange("(b q t u) n -> b t q u n", b=2, t=4, u=8)
        for b in range(2):
            for t in range(4):
                nc.sync.dma_start(w2_raw[:, b, t, :], w2_rows[b, t])
        rel_sb = keep.tile([P, 4, KEPT], F32, name="rel_sb", tag="side_raw", align_bytes=64)
        nc.sync.dma_start(rel_sb[:], rel.rearrange("(i p) j -> p i j", p=P))

        low = [keep.tile([P, S // 2], F32, name="low%d" % i, align_bytes=64) for i in range(3)]
        high = [keep.tile([P, 3 * S // 4 if i == 1 else S // 2], F32, name="high%d" % i, align_bytes=64) for i in range(3)]
        bent = [(low[i][:], high[i][:, 0 : S // 2]) for i in range(3)]

        def features(s):
            b, t = divmod(s, 4)
            halves = bent[2] if s == 0 else bent[s % 2]
            h = ring.tile([P, S], F32, name="h", bufs=3)
            g = per_row[:, b, t : t + 1]
            for lo, hi in FIRST_CHUNKS if s == 0 else BANK_CHUNKS:
                z = psum.tile([P, BANK], F32, name="z", bufs=4)
                for a in range(2):
                    nc.tensor.matmul_mx(
                        out=z[:, 0 : hi - lo],
                        lhsT=w1_codes[b][:, a, t, :].bitcast(FP4X4),
                        lhsT_scale=w1_plane[b][:, a, t, :],
                        rhs=v_words[a][:, lo:hi].bitcast(FP8X4),
                        rhs_scale=v_plane[a][:, lo:hi],
                        start=(a == 0),
                        stop=(a == 1),
                    )
                half, at = divmod(lo, S // 2)
                th = halves[half][:, at : at + hi - lo]
                nc.scalar.activation(out=th, in_=z[:, 0 : hi - lo], func=ACT.Tanh)
                if s == 0:
                    nc.vector.tensor_scalar(h[:, lo:hi], th, g, None, ALU.mult)
            if s > 0:
                for half in range(2):
                    nc.scalar.activation(
                        out=h[:, half * S // 2 : (half + 1) * S // 2], in_=halves[half], func=ACT.Copy, scale=g
                    )
            return h

        lefts = [keep.tile([P, PAIRS], F32, name="left%d" % i) for i in range(2)]
        rights = [keep.tile([P, PAIRS], F32, name="right%d" % t) for t in range(4)]
        lift_last = keep.tile([P, KEPT], F32, name="lift_last")
        a1_ring = [keep.tile([P, PAIRS], F32, name="a1_%d" % t) for t in range(4)]
        late = bent[(SLICES - 1) % 2]

        def a1(s):
            return late[0] if s == SLICES - 1 else a1_ring[s % 4][:]

        def lift(s):
            return lift_last[:] if s == SLICES - 1 else rights[s % 4][:, 0:KEPT]

        def pairs(s, h):
            b, t = divmod(s, 4)
            left = lefts[s % 2][:]
            right = rights[t][:]
            h4 = ring.tile([P, KEPT], F32, name="h4")
            if s + 1 < SLICES:
                nc.vector.tensor_copy(left, h[:].indirect(p1[:]))
                nc.vector.tensor_copy(h4[:], h[:].indirect(p4[:]))
                nc.vector.tensor_tensor(right, h[:].indirect(p2[:]), left, ALU.subtract)
                excess = bent[(s + 1) % 2][1 if s in (0, SLICES - 2) else 0]
                nc.scalar.activation(out=excess, in_=right, func=ACT.Relu)
                nc.gpsimd.tensor_tensor(a1(s), left, excess, ALU.add)
            else:
                nc.vector.tensor_copy(h4[:], h[:].indirect(p4[:]))
                nc.vector.tensor_copy(left, h[:].indirect(p1[:]))
                nc.vector.tensor_copy(right, h[:].indirect(p2[:]))
            nc.scalar.activation(out=lift(s), in_=h4[:], func=ACT.Copy, scale=per_row[:, b, 4 + t : 5 + t], bias=1.0)

        def quantise(grouped, name):
            width = grouped.shape[1] // 4
            codes = keep.tile([P, width], U32, name=name + "_codes", align_bytes=64)
            plane = keep.tile([P, width], U8, name=name + "_plane", align_bytes=64)
            nc.vector.quantize_mx(out=codes[:].bitcast(FP8X4), scales=plane[:], in_=grouped)
            return codes, plane

        def kept(s, lo, hi, into):
            nc.vector.tensor_tensor(into, a1(s).indirect(p3[:, lo // 16 : hi // 16]), lift(s)[:, lo:hi], ALU.mult)

        def place(c, i):
            lo, hi = TAIL_CHUNKS[c]
            width = hi - lo
            per_bank = BANK // width
            first_bank = 4 * lo // BANK
            return first_bank + i // per_bank, (i % per_bank) * width, i % per_bank == 0, i % per_bank == per_bank - 1

        def scores(b, c, w2_q, a2_q, col):
            lo, hi = TAIL_CHUNKS[c]
            for i in range(4):
                bank, at, first, last = place(c, i)
                nc.tensor.matmul_mx(
                    out=out_bank[bank][:, at : at + hi - lo],
                    lhsT=w2_q[0][:, P * i : P * (i + 1)].bitcast(FP8X4),
                    lhsT_scale=w2_q[1][:, P * i : P * (i + 1)],
                    rhs=a2_q[0][:, col : col + hi - lo].bitcast(FP8X4),
                    rhs_scale=a2_q[1][:, col : col + hi - lo],
                    start=(b == 0 and first),
                    stop=(b == 1 and last),
                )

        a2_first = keep.tile([P, 4, KEPT], F32, name="a2_first")
        parts = [keep.tile([P, 4, hi - lo], F32, name="a2_part%d" % lo)[:] for lo, hi in TAIL_CHUNKS[:2]]
        h_next = features(0)
        w2_low = bent[2][1].bitcast(BF16)
        nc.gpsimd.tensor_scalar(
            w2_low.rearrange("p (c t) -> p c t", t=4), w2_raw[:, 0, :, :].rearrange("p t c -> p c t"), 1.0, 0.0, ALU.mult, ALU.add
        )
        for s in range(SLICES):
            h = h_next
            if s + 1 < SLICES:
                h_next = features(s + 1)
            pairs(s, h)
            if s == SLICES - 1:
                a2_low = late[0].bitcast(BF16)
                interleave(nc, a2_low, a2_first[:])
                a2_q = quantise(a2_low, "a2_low")
                for c, (lo, hi) in enumerate(TAIL_CHUNKS):
                    scores(0, c, w2_q[0], a2_q, lo)
                nc.vector.tensor_tensor(a1(s), lefts[s % 2][:], rights[s % 4][:], ALU.max)
            if s < 4:
                kept(s, 0, KEPT, a2_first[:, s, :])
            else:
                for part, (lo, hi) in zip(parts, TAIL_CHUNKS):
                    kept(s, lo, hi, part[:, s - 4, :])
            if s == 0:
                w2_q = [quantise(w2_low, "w2_low")]

        w2_high = late[1].bitcast(BF16)
        interleave(nc, w2_high, w2_raw[:, 1, :, :])
        w2_q.append(quantise(w2_high, "w2_high"))

        out_rows = out.rearrange("(i p) j -> p i j", p=P)
        for c, (lo, hi) in enumerate(TAIL_CHUNKS):
            width = hi - lo
            if c == 0:
                grouped = high[1][:, S // 2 : S // 2 + 2 * width].bitcast(BF16)
            else:
                grouped = keep.tile([P, 4 * width], BF16, name="a2_high%d" % c, align_bytes=64)[:]
            if c == 2:
                parts.append(high[1][:, S // 2 - 2 * width : S // 2 + 2 * width].rearrange("p (t j) -> p t j", t=4))
                for t in range(4):
                    kept(4 + t, lo, hi, parts[2][:, t, :])
            interleave(nc, grouped, parts[c])
            a2_q = quantise(grouped, "a2_high%d" % c)
            scores(1, c, w2_q[1], a2_q, 0)
            per_bank = BANK // width
            for i0 in range(0, 4, per_bank):
                bank = place(c, i0)[0]
                result = keep.tile([P, per_bank, width], F32, name="result%d" % bank)
                nc.vector.tensor_tensor(
                    result[:],
                    out_bank[bank][:].rearrange("p (i j) -> p i j", i=per_bank),
                    rel_sb[:, i0 : i0 + per_bank, lo:hi],
                    ALU.mult,
                )
                nc.sync.dma_start(out_rows[:, i0 : i0 + per_bank, lo:hi], result[:])
